import numpy as np
import ml_dtypes


def mxq(x, axis, fmt="e4m3"):
    dtype, down = {"e4m3": (ml_dtypes.float8_e4m3fn, 7), "e5m2": (ml_dtypes.float8_e5m2, 14)}[fmt]
    v = np.moveaxis(np.asarray(x, np.float32).astype(ml_dtypes.bfloat16).astype(np.float64), axis, -1)
    blocks = v.reshape(v.shape[:-1] + (-1, 32))
    amax = np.abs(blocks).max(-1, keepdims=True)
    byte = np.maximum(np.where(amax > 0, np.frexp(amax)[1] - 1 + 127, 0) - down, 1)
    scale = np.exp2(byte - 127.0)
    codes = (blocks / scale).astype(np.float32).astype(dtype).astype(np.float64)
    return np.moveaxis((codes * scale).reshape(v.shape), -1, axis)


WIDE = False


def mx_kscale(k):
    if not WIDE:
        return np.ones(k)
    levels = np.array([10, -10, 5, -5, 0])
    if k % 512:
        return np.exp2(np.random.permutation(np.resize(levels, k // 32))).repeat(32)
    a = np.empty((k // 512, 16))
    for p in range(k // 512):
        a[p, :8] = np.random.permutation(np.resize(levels, 8))
        for g in range(8):
            far = levels[np.abs(levels - a[p, g]) >= 10]
            a[p, g + 8] = far[np.random.randint(len(far))]
    return np.exp2(a.ravel()).repeat(32)


def f64(x):
    return np.asarray(x).astype(np.float64)


def striped(idx):
    return np.tile(np.asarray(idx).reshape(-1, 16).T, (8, 1)).astype(np.uint16)


def unstriped(offs):
    return offs[:16].T.reshape(-1).astype(np.int64)


E2M1 = np.array([0.0, 0.5, 1.0, 1.5, 2.0, 3.0, 4.0, 6.0, -0.0, -0.5, -1.0, -1.5, -2.0, -3.0, -4.0, -6.0])


def pack_weight(w, fmt):
    k, n = w.shape
    w = f64(np.asarray(w, np.float32).astype(ml_dtypes.bfloat16)).reshape(k // 32, 32, n)
    amax = np.abs(w).max(1)
    if fmt == "e4m3":
        byte = np.frexp(amax)[1] - 1 + 127 - 7
    else:
        mant, ex = np.frexp(amax / 6.0)
        byte = np.where(mant > 0.5, ex, ex - 1) + 127
    byte = np.clip(np.where(amax > 0, byte, 1), 1, 254)
    scaled = (w * np.exp2(127.0 - byte)[:, None, :]).reshape(k, n).astype(np.float32)
    by_word = np.ascontiguousarray(scaled.reshape(k // 512, 128, 4, n).transpose(0, 1, 3, 2))
    if fmt == "e4m3":
        words = by_word.astype(ml_dtypes.float8_e4m3fn).view(np.uint8)
    else:
        c = by_word.astype(ml_dtypes.float4_e2m1fn).view(np.uint8) & 0xF
        words = (c[..., 0::2] | (c[..., 1::2] << 4)).reshape(k // 512, 128, 2 * n)
    return np.ascontiguousarray(words), np.ascontiguousarray(byte.astype(np.uint8).reshape(k // 512, 16, n))


def unpack_weight(words, scales, fmt):
    g, _, n = scales.shape
    words = np.ascontiguousarray(words).reshape(g, 128, n, -1)
    if fmt == "e4m3":
        vals = words.view(ml_dtypes.float8_e4m3fn).astype(np.float64)
    else:
        nib = np.empty((g, 128, n, 4), np.uint8)
        nib[..., 0::2] = words & 0xF
        nib[..., 1::2] = words >> 4
        vals = E2M1[nib]
    vals = vals * np.repeat(np.exp2(scales.astype(np.float64) - 127.0), 8, axis=1)[..., None]
    return vals.transpose(0, 1, 3, 2).reshape(g * 512, n)


def sigmoid(v):
    return 1.0 / (1.0 + np.exp(-v))


K, R, F, T, J, G = 512, 128, 512, 2048, 512, 64


def setup_inputs():
    n = np.random.standard_normal
    idx = np.random.permutation(T)[:J]
    fk = mx_kscale(K)
    ff = mx_kscale(F)
    fj = mx_kscale(J)
    tj = np.ones(T)
    tj[idx] = fj
    tabp = pack_weight(n((K, T)) / fk[:, None], "e2m1")
    return {
        "tab_words": tabp[0],
        "tab_scales": tabp[1],
        "w1": (n((K, R)) * 1 / np.sqrt(K) * fk[:, None]).astype(np.float32),
        "steep": (np.random.uniform(1.0, 4.0, (R, 1))).astype(np.float32),
        "wo": (n((F, R)) * 1 / np.sqrt(F) * ff[:, None]).astype(np.float32),
        "dy": (n((F, G)) / ff[:, None]).astype(np.float32),
        "js": (np.random.uniform(0.5, 2.0, (1, J)) * fj).astype(np.float32),
        "xrows": (n((K, T)) / tj).astype(np.float32),
        "old": (n((K, R)) * 4.0).astype(np.float32),
        "offs": striped(idx),
    }


def reference(tab_words, tab_scales, w1, steep, wo, dy, js, xrows, old, offs):
    idx = unstriped(offs)
    tabu = unpack_weight(tab_words, tab_scales, "e2m1")
    w1q = mxq(f64(w1), 0, "e4m3")
    tabidxg = tabu[:, idx]
    a = w1q.T @ tabidxg
    h1 = np.tanh(a)
    p = sigmoid(a * f64(steep))
    z = p.reshape(R, G, J // G).sum(axis=2)
    woq = mxq(f64(wo), 0, "e4m3")
    dyq = mxq(f64(dy), 0, "e4m3")
    c0 = woq.T @ dyq
    e1 = c0 / z
    r1 = np.repeat(e1, J // G, axis=1)
    dz = c0 * (p * h1).reshape(R, G, J // G).sum(axis=2) / np.square(z) * (-1.0)
    r2 = np.repeat(dz, J // G, axis=1)
    dp = r1 * h1 + r2
    dh1 = r1 * p
    da = dp * p * (1.0 - p) * f64(steep) + dh1 * (1.0 - np.square(h1))
    gs = da * f64(js)
    gt1 = gs.T
    xt = f64(xrows)[:, idx].T
    xtq = mxq(xt, 0, "e4m3")
    gt1q = mxq(gt1, 0, "e4m3")
    gw = xtq.T @ gt1q
    y = gw + f64(old)
    return y

@@ -1,0 +1,201 @@
+from contextlib import ExitStack
+
+import concourse.mybir as mybir
+from concourse.masks import make_identity
+
+K, R, F, T, J, G = 512, 128, 512, 2048, 512, 64
+FLOPS = 2 * K * R * J + 2 * F * R * G + 2 * J * K * R
+
+F32 = mybir.dt.float32
+BF16 = mybir.dt.bfloat16
+I32 = mybir.dt.int32
+U32 = mybir.dt.uint32
+U16 = mybir.dt.uint16
+U8 = mybir.dt.uint8
+FP8X4 = mybir.dt.float8_e4m3fn_x4
+FP4X4 = mybir.dt.float4_e2m1fn_x4
+ACT = mybir.ActivationFunctionType
+ALU = mybir.AluOpType
+AXIS = mybir.AxisListType
+
+P = 128
+PACK = 4
+
+
+def tile_attend_cgroupvote_w_kernel(tc, tab_words, tab_scales, w1, steep, wo, dy, js, xrows, old, offs, out):
+    nc = tc.nc
+    with ExitStack() as ctx:
+        keep = ctx.enter_context(tc.tile_pool(name="keep", bufs=1))
+        psum = ctx.enter_context(tc.psum_pool(name="psum", bufs=1))
+
+        def sbuf(name, shape, dtype):
+            return keep.tile(shape, dtype, name=name, align_bytes=64)
+
+        def quantize(name, grouped, columns):
+            codes = sbuf(name + "_codes", [P, columns], U32)
+            scales = sbuf(name + "_scales", [P, columns], U8)
+            nc.vector.quantize_mx(out=codes[:].bitcast(FP8X4), scales=scales[:], in_=grouped)
+            return codes[:].bitcast(FP8X4), scales[:]
+
+        offsets = keep.tile([P, J // 16], U16, name="offsets")
+        nc.sync.dma_start(offsets[:], offs)
+        words = sbuf("words", [P, T], U16)
+        nc.sync.dma_start(words[:].bitcast(I32), tab_words[0].bitcast(I32))
+        plane = sbuf("plane", [P, T], U8)
+        nc.vector.memset(plane[:].bitcast(I32), 0)
+        for q in range(4):
+            nc.scalar.dma_start(
+                plane[32 * q : 32 * q + 4, :].bitcast(I32), tab_scales[0, 4 * q : 4 * q + 4, :].bitcast(I32)
+            )
+        w1_raw = sbuf("w1_raw", [P, PACK, R], F32)
+        nc.sync.dma_start(w1_raw[:], w1.rearrange("(p t) r -> p t r", t=PACK))
+        steep_col = sbuf("steep_col", [P, 1], F32)
+        js_cols = sbuf("js_cols", [P, PACK], F32)
+        x_view = xrows.rearrange("(p b) c -> p b c", b=PACK)
+        x_raw = [sbuf("x_raw%d" % b, [P, T], F32) for b in range(PACK)]
+        nc.sync.dma_start(x_raw[0][:], x_view[:, 0, :])
+        nc.sync.dma_start(steep_col[:], steep)
+        wo_raw = sbuf("wo_raw", [P, PACK, R], F32)
+        nc.sync.dma_start(wo_raw[:], wo.rearrange("(p t) r -> p t r", t=PACK))
+        dy_raw = sbuf("dy_raw", [P, PACK, G], F32)
+        nc.sync.dma_start(dy_raw[:], dy.rearrange("(p t) g -> p t g", t=PACK))
+        nc.sync.dma_start(js_cols[:], js.rearrange("o (p t) -> (o p) t", t=PACK))
+        for b in range(1, PACK):
+            nc.sync.dma_start(x_raw[b][:], x_view[:, b, :])
+        old_sb = sbuf("old_sb", [P, PACK, R], F32)
+        nc.sync.dma_start(old_sb[:], old.rearrange("(p b) r -> p b r", b=PACK))
+
+        ident = sbuf("ident", [P, P], F32)
+        make_identity(nc, ident[:])
+
+        warm = sbuf("warm", [P, 1], F32)
+        nc.scalar.activation(warm[:], ident[:, 0:1], ACT.Sigmoid)
+
+        w1_grouped = sbuf("w1_grouped", [P, R, PACK], BF16)
+        nc.scalar.copy(w1_grouped[:], w1_raw[:].rearrange("p t r -> p r t"))
+        words_g = sbuf("words_g", [P, J], U16)
+        nc.vector.tensor_copy(words_g[:], words[:].indirect(offsets[:]))
+        plane_g = sbuf("plane_g", [P, J], U8)
+        nc.vector.tensor_copy(plane_g[:], plane[:].indirect(offsets[:]))
+        w1_q, w1_s = quantize("w1", w1_grouped[:].rearrange("p r t -> p (r t)"), R)
+        a_ps = psum.tile([P, J], F32, name="a_ps")
+        nc.tensor.matmul_mx(
+            out=a_ps[:], lhsT=w1_q, lhsT_scale=w1_s, rhs=words_g[:].bitcast(FP4X4), rhs_scale=plane_g[:],
+            start=True, stop=True,
+        )
+
+        def gather_x(b):
+            xg = sbuf("xg%d" % b, [P, J], BF16)
+            nc.vector.tensor_copy(xg[:], x_raw[b][:].indirect(offsets[:]))
+            pairs = xg[:].bitcast(F32)
+            xt_ps = psum.tile([P, 2, P], F32, name="xt_ps%d" % b, tag="xt_ps", bufs=2)
+            for u in range(2):
+                nc.tensor.transpose(xt_ps[:, u, :], pairs[:, u : J // 2 : 2], ident[:])
+            xt = sbuf("xt%d" % b, [P, P, PACK], BF16)
+            nc.scalar.copy(
+                xt[:].rearrange("p k t -> p (k t)").bitcast(F32).rearrange("p (k u) -> p k u", u=2),
+                xt_ps[:].rearrange("p u k -> p k u"),
+            )
+            return xt
+
+        def quantize_x(b, xt):
+            return quantize("xt%d" % b, xt[:].rearrange("p k t -> p (k t)"), P)
+
+        a_dealt = a_ps[:].rearrange("r (s t) -> r t s", t=PACK)
+        p_t = sbuf("p_t", [P, PACK, P], F32)
+        nc.scalar.activation(p_t[:], a_dealt, ACT.Sigmoid, scale=steep_col[:])
+        h_t = sbuf("h_t", [P, PACK, P], F32)
+        nc.scalar.activation(h_t[:], a_dealt, ACT.Tanh)
+        hh_t = sbuf("hh_t", [P, PACK, P], F32)
+        nc.scalar.activation(hh_t[:], h_t[:], ACT.Square)
+
+        xt0 = gather_x(0)
+
+        def flat(t):
+            return t[:].rearrange("r t s -> r (t s)")
+
+        def by_group(t):
+            return t[:].rearrange("r t (g e) -> r g t e", e=2)
+
+        z = sbuf("z", [P, G], F32)
+        nc.vector.tensor_reduce(z[:], by_group(p_t), AXIS.XY, ALU.add)
+        ph_t = sbuf("ph_t", [P, PACK, P], F32)
+        nc.vector.tensor_tensor(flat(ph_t), flat(p_t), flat(h_t), ALU.mult)
+        rz = sbuf("rz", [P, G], F32)
+        nc.vector.reciprocal(rz[:], z[:])
+        s_ph = sbuf("s_ph", [P, G], F32)
+        nc.vector.tensor_reduce(s_ph[:], by_group(ph_t), AXIS.XY, ALU.add)
+        npq = sbuf("npq", [P, PACK, P], F32)
+        nc.vector.scalar_tensor_tensor(flat(npq), flat(p_t), -1.0, flat(p_t), ALU.add, ALU.mult)
+        m = sbuf("m", [P, G], F32)
+        nc.vector.tensor_tensor(m[:], s_ph[:], rz[:], ALU.mult)
+
+        wo_grouped = sbuf("wo_grouped", [P, R, PACK], BF16)
+        nc.scalar.copy(wo_grouped[:], wo_raw[:].rearrange("p t r -> p r t"))
+        dy_grouped = sbuf("dy_grouped", [P, G, PACK], BF16)
+        nc.scalar.copy(dy_grouped[:], dy_raw[:].rearrange("p t g -> p g t"))
+        wo_q, wo_s = quantize("wo", wo_grouped[:].rearrange("p r t -> p (r t)"), R)
+        dy_q, dy_s = quantize("dy", dy_grouped[:].rearrange("p g t -> p (g t)"), G)
+        c0_ps = psum.tile([P, G], F32, name="c0_ps")
+        nc.tensor.matmul_mx(out=c0_ps[:], lhsT=wo_q, lhsT_scale=wo_s, rhs=dy_q, rhs_scale=dy_s, start=True, stop=True)
+
+        term2 = sbuf("term2", [P, PACK, P], F32)
+        nc.vector.scalar_tensor_tensor(flat(term2), flat(hh_t), -1.0, flat(p_t), ALU.add, ALU.mult)
+        centred = sbuf("centred", [P, PACK, P], F32)
+        nc.vector.tensor_tensor(
+            centred[:].rearrange("r t (g e) -> r t g e", e=2),
+            h_t[:].rearrange("r t (g e) -> r t g e", e=2),
+            m[:].rearrange("r (t g e) -> r t g e", t=1, e=1).broadcast_to([P, PACK, G, 2]),
+            ALU.subtract,
+        )
+        ne1 = sbuf("ne1", [P, G, 2], F32)
+        nc.vector.scalar_tensor_tensor(
+            ne1[:],
+            c0_ps[:].rearrange("r (g e) -> r g e", e=1).broadcast_to([P, G, 2]),
+            -1.0,
+            rz[:].rearrange("r (g e) -> r g e", e=1).broadcast_to([P, G, 2]),
+            ALU.mult,
+            ALU.mult,
+        )
+        term1 = sbuf("term1", [P, PACK, P], F32)
+        nc.vector.scalar_tensor_tensor(flat(term1), flat(centred), steep_col[:], flat(npq), ALU.mult, ALU.mult)
+
+        e_ps = psum.tile([P, R], F32, name="e_ps")
+        nc.tensor.transpose(e_ps[:], ne1[:].rearrange("r g e -> r (g e)"), ident[:])
+        factor = sbuf("factor", [P, PACK, R], F32)
+        for t in range(PACK):
+            nc.scalar.activation(factor[:, t, :], e_ps[:], ACT.Copy, scale=js_cols[:, t : t + 1])
+
+        x0_q = quantize_x(0, xt0)
+        xt1 = gather_x(1)
+
+        y_ps = psum.tile([P, PACK, R], F32, name="y_ps")
+        for t in range(PACK):
+            nc.tensor.matmul(y_ps[:, t, :], term2[:, t, :], ident[:], start=True, stop=False, is_transpose=True)
+            nc.tensor.matmul(y_ps[:, t, :], term1[:, t, :], ident[:], start=False, stop=True, is_transpose=True)
+        gt = sbuf("gt", [P, R, PACK], BF16)
+        nc.vector.tensor_tensor(
+            gt[:], y_ps[:].rearrange("p t r -> p r t"), factor[:].rearrange("p t r -> p r t"), ALU.mult
+        )
+        x1_q = quantize_x(1, xt1)
+        xt2 = gather_x(2)
+        gt_q, gt_s = quantize("gt", gt[:].rearrange("p r t -> p (r t)"), R)
+        xt3 = gather_x(3)
+        x2_q = quantize_x(2, xt2)
+
+        out_view = out.rearrange("(p b) r -> p b r", b=PACK)
+        gw_a = psum.tile([P, PACK - 1, R], F32, name="gw_a")
+        for b, (x_q, x_s) in enumerate([x0_q, x1_q, x2_q]):
+            nc.tensor.matmul_mx(
+                out=gw_a[:, b, :], lhsT=x_q, lhsT_scale=x_s, rhs=gt_q, rhs_scale=gt_s, start=True, stop=True
+            )
+        res_a = sbuf("res_a", [P, PACK - 1, R], F32)
+        nc.vector.tensor_tensor(res_a[:], gw_a[:], old_sb[:, 0 : PACK - 1, :], ALU.add)
+        nc.sync.dma_start(out_view[:, 0 : PACK - 1, :], res_a[:])
+
+        x_q, x_s = quantize_x(3, xt3)
+        gw_b = psum.tile([P, R], F32, name="gw_b")
+        nc.tensor.matmul_mx(out=gw_b[:], lhsT=x_q, lhsT_scale=x_s, rhs=gt_q, rhs_scale=gt_s, start=True, stop=True)
+        res_b = sbuf("res_b", [P, R], F32)
+        nc.vector.tensor_tensor(res_b[:], gw_b[:], old_sb[:, PACK - 1, :], ALU.add)
+        nc.sync.dma_start(out_view[:, PACK - 1, :], res_b[:])

@@ -28,11 +28,11 @@ def tile_attend_cgroupvote_w_kernel(tc, tab_words, tab_scales, w1, steep, wo, dy
         keep = ctx.enter_context(tc.tile_pool(name="keep", bufs=1))
         psum = ctx.enter_context(tc.psum_pool(name="psum", bufs=1))
 
-        def sbuf(name, shape, dtype):
-            return keep.tile(shape, dtype, name=name, align_bytes=64)
+        def sbuf(name, shape, dtype, pool=keep, tag=None):
+            return pool.tile(shape, dtype, name=name, tag=tag or name, align_bytes=64)
 
-        def quantize(name, grouped, columns):
-            codes = sbuf(name + "_codes", [P, columns], U32)
+        def quantize(name, grouped, columns, pool=keep, after=None):
+            codes = sbuf(name + "_codes", [P, columns], U32, pool, after)
             scales = sbuf(name + "_scales", [P, columns], U8)
             nc.vector.quantize_mx(out=codes[:].bitcast(FP8X4), scales=scales[:], in_=grouped)
             return codes[:].bitcast(FP8X4), scales[:]
@@ -41,161 +41,173 @@ def tile_attend_cgroupvote_w_kernel(tc, tab_words, tab_scales, w1, steep, wo, dy
         nc.sync.dma_start(offsets[:], offs)
         words = sbuf("words", [P, T], U16)
         nc.sync.dma_start(words[:].bitcast(I32), tab_words[0].bitcast(I32))
-        plane = sbuf("plane", [P, T], U8)
-        nc.vector.memset(plane[:].bitcast(I32), 0)
-        for q in range(4):
-            nc.scalar.dma_start(
-                plane[32 * q : 32 * q + 4, :].bitcast(I32), tab_scales[0, 4 * q : 4 * q + 4, :].bitcast(I32)
-            )
         w1_raw = sbuf("w1_raw", [P, PACK, R], F32)
         nc.sync.dma_start(w1_raw[:], w1.rearrange("(p t) r -> p t r", t=PACK))
         steep_col = sbuf("steep_col", [P, 1], F32)
-        js_cols = sbuf("js_cols", [P, PACK], F32)
-        x_view = xrows.rearrange("(p b) c -> p b c", b=PACK)
-        x_raw = [sbuf("x_raw%d" % b, [P, T], F32) for b in range(PACK)]
-        nc.sync.dma_start(x_raw[0][:], x_view[:, 0, :])
-        nc.sync.dma_start(steep_col[:], steep)
-        wo_raw = sbuf("wo_raw", [P, PACK, R], F32)
+        nc.gpsimd.dma_start(steep_col[:], steep)
+        plane = sbuf("plane", [P, T], U8)
+        nc.vector.memset(plane[:].bitcast(I32), 0)
+        for q in range(4):
+            nc.sync.dma_start(
+                plane[32 * q : 32 * q + 4, :].bitcast(I32), tab_scales[0, 4 * q : 4 * q + 4, :].bitcast(I32)
+            )
+
+        with tc.tile_pool(name="early", bufs=1) as early:
+            warm_in = sbuf("warm_in", [P, 1], F32, early)
+            nc.vector.memset(warm_in[:], 0.0)
+            warm_out = sbuf("warm_out", [P, 1], F32, early)
+            nc.scalar.activation(warm_out[:], warm_in[:], ACT.Sigmoid)
+
+        late = ctx.enter_context(tc.tile_pool(name="late", bufs=1))
+        wo_raw = sbuf("wo_raw", [P, PACK, R], F32, late)
         nc.sync.dma_start(wo_raw[:], wo.rearrange("(p t) r -> p t r", t=PACK))
-        dy_raw = sbuf("dy_raw", [P, PACK, G], F32)
+        dy_raw = sbuf("dy_raw", [P, PACK, G], F32, late)
         nc.sync.dma_start(dy_raw[:], dy.rearrange("(p t) g -> p t g", t=PACK))
+        x_view = xrows.rearrange("(p b) c -> p b c", b=PACK)
+        x_raw = [sbuf("x_raw%d" % b, [P, T], F32, late) for b in range(PACK)]
+        nc.sync.dma_start(x_raw[0][:], x_view[:, 0, :])
+        js_cols = sbuf("js_cols", [P, PACK], F32, late)
         nc.sync.dma_start(js_cols[:], js.rearrange("o (p t) -> (o p) t", t=PACK))
         for b in range(1, PACK):
             nc.sync.dma_start(x_raw[b][:], x_view[:, b, :])
-        old_sb = sbuf("old_sb", [P, PACK, R], F32)
+        old_sb = sbuf("old_sb", [P, PACK, R], F32, late)
         nc.sync.dma_start(old_sb[:], old.rearrange("(p b) r -> p b r", b=PACK))
 
         ident = sbuf("ident", [P, P], F32)
         make_identity(nc, ident[:])
 
-        warm = sbuf("warm", [P, 1], F32)
-        nc.scalar.activation(warm[:], ident[:, 0:1], ACT.Sigmoid)
-
         w1_grouped = sbuf("w1_grouped", [P, R, PACK], BF16)
         nc.scalar.copy(w1_grouped[:], w1_raw[:].rearrange("p t r -> p r t"))
-        words_g = sbuf("words_g", [P, J], U16)
-        nc.vector.tensor_copy(words_g[:], words[:].indirect(offsets[:]))
-        plane_g = sbuf("plane_g", [P, J], U8)
-        nc.vector.tensor_copy(plane_g[:], plane[:].indirect(offsets[:]))
-        w1_q, w1_s = quantize("w1", w1_grouped[:].rearrange("p r t -> p (r t)"), R)
-        a_ps = psum.tile([P, J], F32, name="a_ps")
-        nc.tensor.matmul_mx(
-            out=a_ps[:], lhsT=w1_q, lhsT_scale=w1_s, rhs=words_g[:].bitcast(FP4X4), rhs_scale=plane_g[:],
-            start=True, stop=True,
-        )
-
-        def gather_x(b):
-            xg = sbuf("xg%d" % b, [P, J], BF16)
-            nc.vector.tensor_copy(xg[:], x_raw[b][:].indirect(offsets[:]))
-            pairs = xg[:].bitcast(F32)
-            xt_ps = psum.tile([P, 2, P], F32, name="xt_ps%d" % b, tag="xt_ps", bufs=2)
-            for u in range(2):
-                nc.tensor.transpose(xt_ps[:, u, :], pairs[:, u : J // 2 : 2], ident[:])
-            xt = sbuf("xt%d" % b, [P, P, PACK], BF16)
-            nc.scalar.copy(
-                xt[:].rearrange("p k t -> p (k t)").bitcast(F32).rearrange("p (k u) -> p k u", u=2),
-                xt_ps[:].rearrange("p u k -> p k u"),
-            )
-            return xt
-
-        def quantize_x(b, xt):
-            return quantize("xt%d" % b, xt[:].rearrange("p k t -> p (k t)"), P)
-
-        a_dealt = a_ps[:].rearrange("r (s t) -> r t s", t=PACK)
-        p_t = sbuf("p_t", [P, PACK, P], F32)
-        nc.scalar.activation(p_t[:], a_dealt, ACT.Sigmoid, scale=steep_col[:])
-        h_t = sbuf("h_t", [P, PACK, P], F32)
-        nc.scalar.activation(h_t[:], a_dealt, ACT.Tanh)
-        hh_t = sbuf("hh_t", [P, PACK, P], F32)
-        nc.scalar.activation(hh_t[:], h_t[:], ACT.Square)
-
-        xt0 = gather_x(0)
-
-        def flat(t):
-            return t[:].rearrange("r t s -> r (t s)")
-
-        def by_group(t):
-            return t[:].rearrange("r t (g e) -> r g t e", e=2)
-
-        z = sbuf("z", [P, G], F32)
-        nc.vector.tensor_reduce(z[:], by_group(p_t), AXIS.XY, ALU.add)
-        ph_t = sbuf("ph_t", [P, PACK, P], F32)
-        nc.vector.tensor_tensor(flat(ph_t), flat(p_t), flat(h_t), ALU.mult)
-        rz = sbuf("rz", [P, G], F32)
-        nc.vector.reciprocal(rz[:], z[:])
-        s_ph = sbuf("s_ph", [P, G], F32)
-        nc.vector.tensor_reduce(s_ph[:], by_group(ph_t), AXIS.XY, ALU.add)
-        npq = sbuf("npq", [P, PACK, P], F32)
-        nc.vector.scalar_tensor_tensor(flat(npq), flat(p_t), -1.0, flat(p_t), ALU.add, ALU.mult)
-        m = sbuf("m", [P, G], F32)
-        nc.vector.tensor_tensor(m[:], s_ph[:], rz[:], ALU.mult)
-
         wo_grouped = sbuf("wo_grouped", [P, R, PACK], BF16)
         nc.scalar.copy(wo_grouped[:], wo_raw[:].rearrange("p t r -> p r t"))
         dy_grouped = sbuf("dy_grouped", [P, G, PACK], BF16)
         nc.scalar.copy(dy_grouped[:], dy_raw[:].rearrange("p t g -> p g t"))
+
+        HALF = J // 2
+        a_ps = []
+        for c in range(2):
+            half_offsets = offsets[:, c * HALF // 16 : (c + 1) * HALF // 16]
+            words_g = sbuf("words_g%d" % c, [P, HALF], U16)
+            nc.vector.tensor_copy(words_g[:], words[:].indirect(half_offsets))
+            plane_g = sbuf("plane_g%d" % c, [P, HALF], U8)
+            nc.vector.tensor_copy(plane_g[:], plane[:].indirect(half_offsets))
+            if c == 0:
+                w1_q, w1_s = quantize("w1", w1_grouped[:].rearrange("p r t -> p (r t)"), R)
+            bank = psum.tile([P, HALF], F32, name="a_ps%d" % c)
+            nc.tensor.matmul_mx(
+                out=bank[:], lhsT=w1_q, lhsT_scale=w1_s, rhs=words_g[:].bitcast(FP4X4), rhs_scale=plane_g[:],
+                start=True, stop=True,
+            )
+            a_ps.append(bank)
+
         wo_q, wo_s = quantize("wo", wo_grouped[:].rearrange("p r t -> p (r t)"), R)
         dy_q, dy_s = quantize("dy", dy_grouped[:].rearrange("p g t -> p (g t)"), G)
         c0_ps = psum.tile([P, G], F32, name="c0_ps")
         nc.tensor.matmul_mx(out=c0_ps[:], lhsT=wo_q, lhsT_scale=wo_s, rhs=dy_q, rhs_scale=dy_s, start=True, stop=True)
 
-        term2 = sbuf("term2", [P, PACK, P], F32)
-        nc.vector.scalar_tensor_tensor(flat(term2), flat(hh_t), -1.0, flat(p_t), ALU.add, ALU.mult)
-        centred = sbuf("centred", [P, PACK, P], F32)
-        nc.vector.tensor_tensor(
-            centred[:].rearrange("r t (g e) -> r t g e", e=2),
-            h_t[:].rearrange("r t (g e) -> r t g e", e=2),
-            m[:].rearrange("r (t g e) -> r t g e", t=1, e=1).broadcast_to([P, PACK, G, 2]),
-            ALU.subtract,
-        )
-        ne1 = sbuf("ne1", [P, G, 2], F32)
-        nc.vector.scalar_tensor_tensor(
-            ne1[:],
-            c0_ps[:].rearrange("r (g e) -> r g e", e=1).broadcast_to([P, G, 2]),
-            -1.0,
-            rz[:].rearrange("r (g e) -> r g e", e=1).broadcast_to([P, G, 2]),
-            ALU.mult,
-            ALU.mult,
-        )
-        term1 = sbuf("term1", [P, PACK, P], F32)
-        nc.vector.scalar_tensor_tensor(flat(term1), flat(centred), steep_col[:], flat(npq), ALU.mult, ALU.mult)
+        def gather_x(b, after):
+            xg = sbuf("xg%d" % b, [P, J], BF16, tag=after)
+            nc.vector.tensor_copy(xg[:], x_raw[b][:].indirect(offsets[:]))
+            return xg
 
-        e_ps = psum.tile([P, R], F32, name="e_ps")
-        nc.tensor.transpose(e_ps[:], ne1[:].rearrange("r g e -> r (g e)"), ident[:])
+        def turn_x(b, xg, xt, bank_tag=None):
+            pairs = xg[:].bitcast(F32)
+            xt_ps = psum.tile([P, 2, P], F32, name="xt_ps%d" % b, tag=bank_tag or "xt_ps%d" % b)
+            for u in range(2):
+                nc.tensor.transpose(xt_ps[:, u, :], pairs[:, u : J // 2 : 2], ident[:])
+            nc.scalar.copy(
+                xt.bitcast(F32).rearrange("p (k u) -> p k u", u=2),
+                xt_ps[:].rearrange("p u k -> p k u"),
+            )
+
+        def flat(t):
+            return t[:].rearrange("r t s -> r (t s)")
+
+        def twice(ap):
+            return ap.rearrange("r (g e) -> r g e", e=1).broadcast_to([P, G, 2])
+
+        def over_places(t):
+            return t[:].rearrange("r (t g) e -> r t (g e)", t=1).broadcast_to([P, PACK, P])
+
+        p_t = sbuf("p_t", [P, PACK, P], F32, late, "dy_raw")
+        h_t = sbuf("h_t", [P, PACK, P], F32)
+        ph_t = sbuf("ph_t", [P, PACK, P], F32)
+        z = sbuf("z", [P, G], F32)
+        s_ph = sbuf("s_ph", [P, G], F32)
+        rz = sbuf("rz", [P, G], F32)
+        for c in range(2):
+            cols = slice(c * P // 2, (c + 1) * P // 2)
+            groups = slice(c * G // 2, (c + 1) * G // 2)
+            a_dealt = a_ps[c][:].rearrange("r (s t) -> r t s", t=PACK)
+            nc.scalar.activation(p_t[:, :, cols], a_dealt, ACT.Sigmoid, scale=steep_col[:])
+            nc.scalar.activation(h_t[:, :, cols], a_dealt, ACT.Tanh)
+            nc.vector.tensor_reduce(
+                z[:, groups], p_t[:, :, cols].rearrange("r t (g e) -> r g t e", e=2), AXIS.XY, ALU.add
+            )
+            nc.vector.tensor_tensor(ph_t[:, :, cols], p_t[:, :, cols], h_t[:, :, cols], ALU.mult)
+            nc.vector.reciprocal(rz[:, groups], z[:, groups])
+            nc.vector.tensor_reduce(
+                s_ph[:, groups], ph_t[:, :, cols].rearrange("r t (g e) -> r g t e", e=2), AXIS.XY, ALU.add
+            )
+        hh_t = sbuf("hh_t", [P, PACK, P], F32)
+        nc.scalar.activation(hh_t[:], h_t[:], ACT.Square)
+        x0_bf16 = sbuf("x0_bf16", [P, T], BF16, tag="words_g1")
+        nc.scalar.activation(x0_bf16[:], x_raw[0][:], ACT.Copy)
+        xg0 = sbuf("xg0", [P, J], BF16)
+        nc.scalar.activation(xg0[:], x0_bf16[:].indirect(offsets[:]), ACT.Copy)
+
+        ne1 = sbuf("ne1", [P, G, 2], F32)
+        nc.vector.scalar_tensor_tensor(ne1[:], twice(c0_ps[:]), -1.0, twice(rz[:]), ALU.mult, ALU.mult)
+        ms = sbuf("ms", [P, G, 2], F32)
+        nc.vector.scalar_tensor_tensor(ms[:], twice(s_ph[:]), steep_col[:], twice(rz[:]), ALU.mult, ALU.mult)
+        centred = sbuf("centred", [P, PACK, P], F32)
+        nc.vector.scalar_tensor_tensor(centred[:], h_t[:], steep_col[:], over_places(ms), ALU.mult, ALU.subtract)
+        pe = sbuf("pe", [P, PACK, P], F32)
+        nc.vector.tensor_tensor(pe[:], p_t[:], over_places(ne1), ALU.mult)
+        term = sbuf("term", [P, PACK, P], F32)
+        nc.vector.scalar_tensor_tensor(flat(term), flat(p_t), -1.0, flat(centred), ALU.add, ALU.mult)
+
+        xg1 = gather_x(1, "ms")
+        pe_ps = psum.tile([P, PACK, R], F32, name="pe_ps", tag="a_ps0")
+        for t in range(PACK):
+            nc.tensor.transpose(pe_ps[:, t, :], pe[:, t, :], ident[:])
+        y_ps = psum.tile([P, PACK, R], F32, name="y_ps", tag="a_ps1")
+        for t in range(PACK):
+            nc.tensor.matmul(y_ps[:, t, :], hh_t[:, t, :], ident[:], start=True, stop=False, is_transpose=True)
+            nc.tensor.matmul(y_ps[:, t, :], term[:, t, :], ident[:], start=False, stop=True, is_transpose=True)
         factor = sbuf("factor", [P, PACK, R], F32)
         for t in range(PACK):
-            nc.scalar.activation(factor[:, t, :], e_ps[:], ACT.Copy, scale=js_cols[:, t : t + 1])
+            nc.scalar.activation(factor[:, t, :], pe_ps[:, t, :], ACT.Copy, scale=js_cols[:, t : t + 1])
 
-        x0_q = quantize_x(0, xt0)
-        xt1 = gather_x(1)
 
-        y_ps = psum.tile([P, PACK, R], F32, name="y_ps")
-        for t in range(PACK):
-            nc.tensor.matmul(y_ps[:, t, :], term2[:, t, :], ident[:], start=True, stop=False, is_transpose=True)
-            nc.tensor.matmul(y_ps[:, t, :], term1[:, t, :], ident[:], start=False, stop=True, is_transpose=True)
-        gt = sbuf("gt", [P, R, PACK], BF16)
-        nc.vector.tensor_tensor(
-            gt[:], y_ps[:].rearrange("p t r -> p r t"), factor[:].rearrange("p t r -> p r t"), ALU.mult
+        xt01 = sbuf("xt01", [P, 2 * J], BF16)
+        xt2 = sbuf("xt2", [P, J], BF16)
+        xt3 = sbuf("xt3", [P, J], BF16)
+        turn_x(1, xg1, xt01[:, J : 2 * J])
+        turn_x(0, xg0, xt01[:, 0:J], "a_ps0")
+        turn_x(2, gather_x(2, "centred"), xt2[:])
+        turn_x(3, gather_x(3, "ne1"), xt3[:])
+        gt = sbuf("gt", [P, R, PACK], BF16, late, "x_raw2")
+        nc.vector.scalar_tensor_tensor(
+            gt[:], y_ps[:].rearrange("p t r -> p r t"), -1.0, factor[:].rearrange("p t r -> p r t"), ALU.add, ALU.mult
         )
-        x1_q = quantize_x(1, xt1)
-        xt2 = gather_x(2)
+        x01_q, x01_s = quantize("x01", xt01[:], 2 * P, late, "x_raw3")
         gt_q, gt_s = quantize("gt", gt[:].rearrange("p r t -> p (r t)"), R)
-        xt3 = gather_x(3)
-        x2_q = quantize_x(2, xt2)
+        x2_q, x2_s = quantize("x2", xt2[:], P, keep, "xt01")
 
         out_view = out.rearrange("(p b) r -> p b r", b=PACK)
         gw_a = psum.tile([P, PACK - 1, R], F32, name="gw_a")
-        for b, (x_q, x_s) in enumerate([x0_q, x1_q, x2_q]):
+        for b, (x_q, x_s) in enumerate([(x01_q[:, 0:P], x01_s[:, 0:P]), (x01_q[:, P:], x01_s[:, P:]), (x2_q, x2_s)]):
             nc.tensor.matmul_mx(
                 out=gw_a[:, b, :], lhsT=x_q, lhsT_scale=x_s, rhs=gt_q, rhs_scale=gt_s, start=True, stop=True
             )
+        x_q, x_s = quantize("x3", xt3[:], P)
         res_a = sbuf("res_a", [P, PACK - 1, R], F32)
         nc.vector.tensor_tensor(res_a[:], gw_a[:], old_sb[:, 0 : PACK - 1, :], ALU.add)
         nc.sync.dma_start(out_view[:, 0 : PACK - 1, :], res_a[:])
 
-        x_q, x_s = quantize_x(3, xt3)
         gw_b = psum.tile([P, R], F32, name="gw_b")
         nc.tensor.matmul_mx(out=gw_b[:], lhsT=x_q, lhsT_scale=x_s, rhs=gt_q, rhs_scale=gt_s, start=True, stop=True)
         res_b = sbuf("res_b", [P, R], F32)
         nc.vector.tensor_tensor(res_b[:], gw_b[:], old_sb[:, PACK - 1, :], ALU.add)
-        nc.sync.dma_start(out_view[:, PACK - 1, :], res_b[:])
+        nc.scalar.dma_start(out_view[:, PACK - 1, :], res_b[:])

@@ -37,6 +37,11 @@ def tile_attend_cgroupvote_w_kernel(tc, tab_words, tab_scales, w1, steep, wo, dy
             nc.vector.quantize_mx(out=codes[:].bitcast(FP8X4), scales=scales[:], in_=grouped)
             return codes[:].bitcast(FP8X4), scales[:]
 
+        def interleave(grouped, raw):
+            nc.scalar.copy(
+                grouped[:].rearrange("p (c i) t -> p c t i", i=4), raw[:].rearrange("p t (c i) -> p c t i", i=4)
+            )
+
         offsets = keep.tile([P, J // 16], U16, name="offsets")
         nc.sync.dma_start(offsets[:], offs)
         words = sbuf("words", [P, T], U16)
@@ -48,9 +53,7 @@ def tile_attend_cgroupvote_w_kernel(tc, tab_words, tab_scales, w1, steep, wo, dy
         plane = sbuf("plane", [P, T], U8)
         nc.vector.memset(plane[:].bitcast(I32), 0)
         for q in range(4):
-            nc.sync.dma_start(
-                plane[32 * q : 32 * q + 4, :].bitcast(I32), tab_scales[0, 4 * q : 4 * q + 4, :].bitcast(I32)
-            )
+            nc.sync.dma_start(plane[q:P:32, :].bitcast(I32), tab_scales[0, q:16:4, :].bitcast(I32))
 
         with tc.tile_pool(name="early", bufs=1) as early:
             warm_in = sbuf("warm_in", [P, 1], F32, early)
@@ -65,10 +68,10 @@ def tile_attend_cgroupvote_w_kernel(tc, tab_words, tab_scales, w1, steep, wo, dy
         nc.sync.dma_start(dy_raw[:], dy.rearrange("(p t) g -> p t g", t=PACK))
         x_view = xrows.rearrange("(p b) c -> p b c", b=PACK)
         x_raw = [sbuf("x_raw%d" % b, [P, T], F32, late) for b in range(PACK)]
-        nc.sync.dma_start(x_raw[0][:], x_view[:, 0, :])
+        nc.sync.dma_start(x_raw[3][:], x_view[:, 3, :])
         js_cols = sbuf("js_cols", [P, PACK], F32, late)
-        nc.sync.dma_start(js_cols[:], js.rearrange("o (p t) -> (o p) t", t=PACK))
-        for b in range(1, PACK):
+        nc.gpsimd.dma_start(js_cols[:], js.rearrange("o (p t) -> (o p) t", t=PACK))
+        for b in range(PACK - 1):
             nc.sync.dma_start(x_raw[b][:], x_view[:, b, :])
         old_sb = sbuf("old_sb", [P, PACK, R], F32, late)
         nc.sync.dma_start(old_sb[:], old.rearrange("(p b) r -> p b r", b=PACK))
@@ -77,11 +80,11 @@ def tile_attend_cgroupvote_w_kernel(tc, tab_words, tab_scales, w1, steep, wo, dy
         make_identity(nc, ident[:])
 
         w1_grouped = sbuf("w1_grouped", [P, R, PACK], BF16)
-        nc.scalar.copy(w1_grouped[:], w1_raw[:].rearrange("p t r -> p r t"))
+        interleave(w1_grouped, w1_raw)
         wo_grouped = sbuf("wo_grouped", [P, R, PACK], BF16)
-        nc.scalar.copy(wo_grouped[:], wo_raw[:].rearrange("p t r -> p r t"))
+        interleave(wo_grouped, wo_raw)
         dy_grouped = sbuf("dy_grouped", [P, G, PACK], BF16)
-        nc.scalar.copy(dy_grouped[:], dy_raw[:].rearrange("p t g -> p g t"))
+        interleave(dy_grouped, dy_raw)
 
         HALF = J // 2
         a_ps = []
@@ -151,10 +154,10 @@ def tile_attend_cgroupvote_w_kernel(tc, tab_words, tab_scales, w1, steep, wo, dy
             )
         hh_t = sbuf("hh_t", [P, PACK, P], F32)
         nc.scalar.activation(hh_t[:], h_t[:], ACT.Square)
-        x0_bf16 = sbuf("x0_bf16", [P, T], BF16, tag="words_g1")
-        nc.scalar.activation(x0_bf16[:], x_raw[0][:], ACT.Copy)
-        xg0 = sbuf("xg0", [P, J], BF16)
-        nc.scalar.activation(xg0[:], x0_bf16[:].indirect(offsets[:]), ACT.Copy)
+        x3_bf16 = sbuf("x3_bf16", [P, T], BF16, tag="words_g1")
+        nc.scalar.activation(x3_bf16[:], x_raw[3][:], ACT.Copy)
+        xg3 = sbuf("xg3", [P, J], BF16)
+        nc.scalar.activation(xg3[:], x3_bf16[:].indirect(offsets[:]), ACT.Copy)
 
         ne1 = sbuf("ne1", [P, G, 2], F32)
         nc.vector.scalar_tensor_tensor(ne1[:], twice(c0_ps[:]), -1.0, twice(rz[:]), ALU.mult, ALU.mult)
@@ -167,47 +170,44 @@ def tile_attend_cgroupvote_w_kernel(tc, tab_words, tab_scales, w1, steep, wo, dy
         term = sbuf("term", [P, PACK, P], F32)
         nc.vector.scalar_tensor_tensor(flat(term), flat(p_t), -1.0, flat(centred), ALU.add, ALU.mult)
 
-        xg1 = gather_x(1, "ms")
+        xg0 = gather_x(0, "ms")
         pe_ps = psum.tile([P, PACK, R], F32, name="pe_ps", tag="a_ps0")
         for t in range(PACK):
             nc.tensor.transpose(pe_ps[:, t, :], pe[:, t, :], ident[:])
         y_ps = psum.tile([P, PACK, R], F32, name="y_ps", tag="a_ps1")
         for t in range(PACK):
-            nc.tensor.matmul(y_ps[:, t, :], hh_t[:, t, :], ident[:], start=True, stop=False, is_transpose=True)
-            nc.tensor.matmul(y_ps[:, t, :], term[:, t, :], ident[:], start=False, stop=True, is_transpose=True)
+            nc.tensor.matmul(y_ps[:, t, :], hh_t[:, t, :], ident[:], start=t == 0, stop=False, is_transpose=True)
+        for t in range(PACK):
+            nc.tensor.matmul(y_ps[:, t, :], term[:, t, :], ident[:], start=False, stop=t == PACK - 1, is_transpose=True)
         factor = sbuf("factor", [P, PACK, R], F32)
         for t in range(PACK):
             nc.scalar.activation(factor[:, t, :], pe_ps[:, t, :], ACT.Copy, scale=js_cols[:, t : t + 1])
 
 
         xt01 = sbuf("xt01", [P, 2 * J], BF16)
-        xt2 = sbuf("xt2", [P, J], BF16)
-        xt3 = sbuf("xt3", [P, J], BF16)
-        turn_x(1, xg1, xt01[:, J : 2 * J])
-        turn_x(0, xg0, xt01[:, 0:J], "a_ps0")
-        turn_x(2, gather_x(2, "centred"), xt2[:])
-        turn_x(3, gather_x(3, "ne1"), xt3[:])
+        xt23 = sbuf("xt23", [P, 2 * J], BF16)
+        turn_x(0, xg0, xt01[:, 0:J])
+        turn_x(1, gather_x(1, "centred"), xt01[:, J : 2 * J])
+        turn_x(3, xg3, xt23[:, J : 2 * J], "a_ps0")
+        turn_x(2, gather_x(2, "ne1"), xt23[:, 0:J])
         gt = sbuf("gt", [P, R, PACK], BF16, late, "x_raw2")
         nc.vector.scalar_tensor_tensor(
             gt[:], y_ps[:].rearrange("p t r -> p r t"), -1.0, factor[:].rearrange("p t r -> p r t"), ALU.add, ALU.mult
         )
-        x01_q, x01_s = quantize("x01", xt01[:], 2 * P, late, "x_raw3")
+        x01 = quantize("x01", xt01[:], 2 * P, keep, "factor")
         gt_q, gt_s = quantize("gt", gt[:].rearrange("p r t -> p (r t)"), R)
-        x2_q, x2_s = quantize("x2", xt2[:], P, keep, "xt01")
+        x23 = quantize("x23", xt23[:], 2 * P, keep, "xt01")
 
         out_view = out.rearrange("(p b) r -> p b r", b=PACK)
-        gw_a = psum.tile([P, PACK - 1, R], F32, name="gw_a")
-        for b, (x_q, x_s) in enumerate([(x01_q[:, 0:P], x01_s[:, 0:P]), (x01_q[:, P:], x01_s[:, P:]), (x2_q, x2_s)]):
-            nc.tensor.matmul_mx(
-                out=gw_a[:, b, :], lhsT=x_q, lhsT_scale=x_s, rhs=gt_q, rhs_scale=gt_s, start=True, stop=True
-            )
-        x_q, x_s = quantize("x3", xt3[:], P)
-        res_a = sbuf("res_a", [P, PACK - 1, R], F32)
-        nc.vector.tensor_tensor(res_a[:], gw_a[:], old_sb[:, 0 : PACK - 1, :], ALU.add)
-        nc.sync.dma_start(out_view[:, 0 : PACK - 1, :], res_a[:])
-
-        gw_b = psum.tile([P, R], F32, name="gw_b")
-        nc.tensor.matmul_mx(out=gw_b[:], lhsT=x_q, lhsT_scale=x_s, rhs=gt_q, rhs_scale=gt_s, start=True, stop=True)
-        res_b = sbuf("res_b", [P, R], F32)
-        nc.vector.tensor_tensor(res_b[:], gw_b[:], old_sb[:, PACK - 1, :], ALU.add)
-        nc.scalar.dma_start(out_view[:, PACK - 1, :], res_b[:])
+        for pair, (x_q, x_s), queue in ((0, x01, nc.sync), (1, x23, nc.scalar)):
+            blocks = slice(2 * pair, 2 * pair + 2)
+            gw = psum.tile([P, 2, R], F32, name="gw%d" % pair)
+            for i in range(2):
+                cols = slice(i * P, (i + 1) * P)
+                nc.tensor.matmul_mx(
+                    out=gw[:, i, :], lhsT=x_q[:, cols], lhsT_scale=x_s[:, cols], rhs=gt_q, rhs_scale=gt_s,
+                    start=True, stop=True,
+                )
+            res = sbuf("res%d" % pair, [P, 2, R], F32)
+            nc.vector.tensor_tensor(res[:], gw[:], old_sb[:, blocks, :], ALU.add)
+            queue.dma_start(out_view[:, blocks, :], res[:])

@@ -68,10 +68,10 @@ def tile_attend_cgroupvote_w_kernel(tc, tab_words, tab_scales, w1, steep, wo, dy
         nc.sync.dma_start(dy_raw[:], dy.rearrange("(p t) g -> p t g", t=PACK))
         x_view = xrows.rearrange("(p b) c -> p b c", b=PACK)
         x_raw = [sbuf("x_raw%d" % b, [P, T], F32, late) for b in range(PACK)]
-        nc.sync.dma_start(x_raw[3][:], x_view[:, 3, :])
+        nc.sync.dma_start(x_raw[2][:], x_view[:, 2, :])
         js_cols = sbuf("js_cols", [P, PACK], F32, late)
         nc.gpsimd.dma_start(js_cols[:], js.rearrange("o (p t) -> (o p) t", t=PACK))
-        for b in range(PACK - 1):
+        for b in (0, 1, 3):
             nc.sync.dma_start(x_raw[b][:], x_view[:, b, :])
         old_sb = sbuf("old_sb", [P, PACK, R], F32, late)
         nc.sync.dma_start(old_sb[:], old.rearrange("(p b) r -> p b r", b=PACK))
@@ -123,15 +123,14 @@ def tile_attend_cgroupvote_w_kernel(tc, tab_words, tab_scales, w1, steep, wo, dy
                 xt_ps[:].rearrange("p u k -> p k u"),
             )
 
-        def flat(t):
-            return t[:].rearrange("r t s -> r (t s)")
-
         def twice(ap):
             return ap.rearrange("r (g e) -> r g e", e=1).broadcast_to([P, G, 2])
 
         def over_places(t):
             return t[:].rearrange("r (t g) e -> r t (g e)", t=1).broadcast_to([P, PACK, P])
 
+        neg_steep = sbuf("neg_steep", [P, 1], F32)
+        nc.gpsimd.tensor_scalar(neg_steep[:], steep_col[:], -1.0, 0.0, ALU.mult, ALU.add)
         p_t = sbuf("p_t", [P, PACK, P], F32, late, "dy_raw")
         h_t = sbuf("h_t", [P, PACK, P], F32)
         ph_t = sbuf("ph_t", [P, PACK, P], F32)
@@ -147,67 +146,76 @@ def tile_attend_cgroupvote_w_kernel(tc, tab_words, tab_scales, w1, steep, wo, dy
             nc.vector.tensor_reduce(
                 z[:, groups], p_t[:, :, cols].rearrange("r t (g e) -> r g t e", e=2), AXIS.XY, ALU.add
             )
-            nc.vector.tensor_tensor(ph_t[:, :, cols], p_t[:, :, cols], h_t[:, :, cols], ALU.mult)
+            nc.vector.scalar_tensor_tensor(
+                ph_t[:, :, cols], p_t[:, :, cols], steep_col[:], h_t[:, :, cols], ALU.mult, ALU.mult
+            )
             nc.vector.reciprocal(rz[:, groups], z[:, groups])
             nc.vector.tensor_reduce(
                 s_ph[:, groups], ph_t[:, :, cols].rearrange("r t (g e) -> r g t e", e=2), AXIS.XY, ALU.add
             )
         hh_t = sbuf("hh_t", [P, PACK, P], F32)
         nc.scalar.activation(hh_t[:], h_t[:], ACT.Square)
-        x3_bf16 = sbuf("x3_bf16", [P, T], BF16, tag="words_g1")
-        nc.scalar.activation(x3_bf16[:], x_raw[3][:], ACT.Copy)
-        xg3 = sbuf("xg3", [P, J], BF16)
-        nc.scalar.activation(xg3[:], x3_bf16[:].indirect(offsets[:]), ACT.Copy)
+        nsh_t = sbuf("nsh_t", [P, PACK, P], F32)
+        nc.scalar.activation(nsh_t[:], h_t[:], ACT.Copy, scale=neg_steep[:])
+        x2_bf16 = sbuf("x2_bf16", [P, T], BF16, tag="words_g1")
+        nc.scalar.activation(x2_bf16[:], x_raw[2][:], ACT.Copy)
 
         ne1 = sbuf("ne1", [P, G, 2], F32)
         nc.vector.scalar_tensor_tensor(ne1[:], twice(c0_ps[:]), -1.0, twice(rz[:]), ALU.mult, ALU.mult)
         ms = sbuf("ms", [P, G, 2], F32)
-        nc.vector.scalar_tensor_tensor(ms[:], twice(s_ph[:]), steep_col[:], twice(rz[:]), ALU.mult, ALU.mult)
-        centred = sbuf("centred", [P, PACK, P], F32)
-        nc.vector.scalar_tensor_tensor(centred[:], h_t[:], steep_col[:], over_places(ms), ALU.mult, ALU.subtract)
+        nc.vector.scalar_tensor_tensor(ms[:], twice(s_ph[:]), -1.0, twice(rz[:]), ALU.mult, ALU.mult)
         pe = sbuf("pe", [P, PACK, P], F32)
         nc.vector.tensor_tensor(pe[:], p_t[:], over_places(ne1), ALU.mult)
         term = sbuf("term", [P, PACK, P], F32)
-        nc.vector.scalar_tensor_tensor(flat(term), flat(p_t), -1.0, flat(centred), ALU.add, ALU.mult)
+        nc.vector.scalar_tensor_tensor(term[:], p_t[:], -1.0, over_places(ms), ALU.add, ALU.mult)
 
-        xg0 = gather_x(0, "ms")
+        xg0 = gather_x(0, "s_ph")
         pe_ps = psum.tile([P, PACK, R], F32, name="pe_ps", tag="a_ps0")
         for t in range(PACK):
             nc.tensor.transpose(pe_ps[:, t, :], pe[:, t, :], ident[:])
         y_ps = psum.tile([P, PACK, R], F32, name="y_ps", tag="a_ps1")
-        for t in range(PACK):
-            nc.tensor.matmul(y_ps[:, t, :], hh_t[:, t, :], ident[:], start=t == 0, stop=False, is_transpose=True)
-        for t in range(PACK):
-            nc.tensor.matmul(y_ps[:, t, :], term[:, t, :], ident[:], start=False, stop=t == PACK - 1, is_transpose=True)
+        addends = [hh_t, ph_t, nsh_t, term]
+        for i, addend in enumerate(addends):
+            for t in range(PACK):
+                nc.tensor.matmul(
+                    y_ps[:, t, :], addend[:, t, :], ident[:], is_transpose=True,
+                    start=i == 0 and t == 0, stop=i == len(addends) - 1 and t == PACK - 1,
+                )
         factor = sbuf("factor", [P, PACK, R], F32)
         for t in range(PACK):
             nc.scalar.activation(factor[:, t, :], pe_ps[:, t, :], ACT.Copy, scale=js_cols[:, t : t + 1])
 
 
+        xg2 = sbuf("xg2", [P, J], BF16, tag="pe")
+        nc.scalar.activation(xg2[:], x2_bf16[:].indirect(offsets[:]), ACT.Copy)
+
         xt01 = sbuf("xt01", [P, 2 * J], BF16)
-        xt23 = sbuf("xt23", [P, 2 * J], BF16)
+        xt2 = sbuf("xt2", [P, J], BF16)
+        xt3 = sbuf("xt3", [P, J], BF16)
         turn_x(0, xg0, xt01[:, 0:J])
-        turn_x(1, gather_x(1, "centred"), xt01[:, J : 2 * J])
-        turn_x(3, xg3, xt23[:, J : 2 * J], "a_ps0")
-        turn_x(2, gather_x(2, "ne1"), xt23[:, 0:J])
-        gt = sbuf("gt", [P, R, PACK], BF16, late, "x_raw2")
+        turn_x(1, gather_x(1, "ms"), xt01[:, J : 2 * J])
+        turn_x(2, xg2, xt2[:], "a_ps0")
+        gt = sbuf("gt", [P, R, PACK], BF16, late, "x_raw1")
         nc.vector.scalar_tensor_tensor(
             gt[:], y_ps[:].rearrange("p t r -> p r t"), -1.0, factor[:].rearrange("p t r -> p r t"), ALU.add, ALU.mult
         )
-        x01 = quantize("x01", xt01[:], 2 * P, keep, "factor")
-        gt_q, gt_s = quantize("gt", gt[:].rearrange("p r t -> p (r t)"), R)
-        x23 = quantize("x23", xt23[:], 2 * P, keep, "xt01")
+        turn_x(3, gather_x(3, "ne1"), xt3[:])
+        gt_q, gt_s = quantize("gt", gt[:].rearrange("p r t -> p (r t)"), R, late, "x_raw3")
+        x01_q, x01_s = quantize("x01", xt01[:], 2 * P, late, "x_raw1")
+        x2_q, x2_s = quantize("x2", xt2[:], P, keep, "xt01")
+        x3_q, x3_s = quantize("x3", xt3[:], P)
 
         out_view = out.rearrange("(p b) r -> p b r", b=PACK)
-        for pair, (x_q, x_s), queue in ((0, x01, nc.sync), (1, x23, nc.scalar)):
-            blocks = slice(2 * pair, 2 * pair + 2)
-            gw = psum.tile([P, 2, R], F32, name="gw%d" % pair)
-            for i in range(2):
-                cols = slice(i * P, (i + 1) * P)
-                nc.tensor.matmul_mx(
-                    out=gw[:, i, :], lhsT=x_q[:, cols], lhsT_scale=x_s[:, cols], rhs=gt_q, rhs_scale=gt_s,
-                    start=True, stop=True,
-                )
-            res = sbuf("res%d" % pair, [P, 2, R], F32)
-            nc.vector.tensor_tensor(res[:], gw[:], old_sb[:, blocks, :], ALU.add)
-            queue.dma_start(out_view[:, blocks, :], res[:])
+        gw_a = psum.tile([P, PACK - 1, R], F32, name="gw_a")
+        for b, (x_q, x_s) in enumerate([(x01_q[:, 0:P], x01_s[:, 0:P]), (x01_q[:, P:], x01_s[:, P:]), (x2_q, x2_s)]):
+            nc.tensor.matmul_mx(
+                out=gw_a[:, b, :], lhsT=x_q, lhsT_scale=x_s, rhs=gt_q, rhs_scale=gt_s, start=True, stop=True
+            )
+        gw_b = psum.tile([P, R], F32, name="gw_b")
+        nc.tensor.matmul_mx(out=gw_b[:], lhsT=x3_q, lhsT_scale=x3_s, rhs=gt_q, rhs_scale=gt_s, start=True, stop=True)
+        res_a = sbuf("res_a", [P, PACK - 1, R], F32, tag="xt3")
+        nc.vector.tensor_tensor(res_a[:], gw_a[:], old_sb[:, 0 : PACK - 1, :], ALU.add)
+        nc.sync.dma_start(out_view[:, 0 : PACK - 1, :], res_a[:])
+        res_b = sbuf("res_b", [P, R], F32)
+        nc.vector.tensor_tensor(res_b[:], gw_b[:], old_sb[:, PACK - 1, :], ALU.add)
+        nc.scalar.dma_start(out_view[:, PACK - 1, :], res_b[:])

from contextlib import ExitStack

import concourse.mybir as mybir
from concourse.masks import make_identity

K, R, F, T, J, G = 512, 128, 512, 2048, 512, 64
FLOPS = 2 * K * R * J + 2 * F * R * G + 2 * J * K * R

F32 = mybir.dt.float32
BF16 = mybir.dt.bfloat16
I32 = mybir.dt.int32
U32 = mybir.dt.uint32
U16 = mybir.dt.uint16
U8 = mybir.dt.uint8
FP8X4 = mybir.dt.float8_e4m3fn_x4
FP4X4 = mybir.dt.float4_e2m1fn_x4
ACT = mybir.ActivationFunctionType
ALU = mybir.AluOpType
AXIS = mybir.AxisListType

P = 128
PACK = 4


def tile_attend_cgroupvote_w_kernel(tc, tab_words, tab_scales, w1, steep, wo, dy, js, xrows, old, offs, out):
    nc = tc.nc
    with ExitStack() as ctx:
        keep = ctx.enter_context(tc.tile_pool(name="keep", bufs=1))
        psum = ctx.enter_context(tc.psum_pool(name="psum", bufs=1))

        def sbuf(name, shape, dtype, pool=keep, tag=None):
            return pool.tile(shape, dtype, name=name, tag=tag or name, align_bytes=64)

        def quantize(name, grouped, columns, pool=keep, after=None):
            codes = sbuf(name + "_codes", [P, columns], U32, pool, after)
            scales = sbuf(name + "_scales", [P, columns], U8)
            nc.vector.quantize_mx(out=codes[:].bitcast(FP8X4), scales=scales[:], in_=grouped)
            return codes[:].bitcast(FP8X4), scales[:]

        def interleave(grouped, raw):
            nc.scalar.copy(
                grouped[:].rearrange("p (c i) t -> p c t i", i=4), raw[:].rearrange("p t (c i) -> p c t i", i=4)
            )

        offsets = keep.tile([P, J // 16], U16, name="offsets")
        nc.sync.dma_start(offsets[:], offs)
        words = sbuf("words", [P, T], U16)
        nc.sync.dma_start(words[:].bitcast(I32), tab_words[0].bitcast(I32))
        w1_raw = sbuf("w1_raw", [P, PACK, R], F32)
        nc.sync.dma_start(w1_raw[:], w1.rearrange("(p t) r -> p t r", t=PACK))
        steep_col = sbuf("steep_col", [P, 1], F32)
        nc.gpsimd.dma_start(steep_col[:], steep)
        plane = sbuf("plane", [P, T], U8)
        nc.vector.memset(plane[:].bitcast(I32), 0)
        for q in range(4):
            nc.sync.dma_start(plane[q:P:32, :].bitcast(I32), tab_scales[0, q:16:4, :].bitcast(I32))

        with tc.tile_pool(name="early", bufs=1) as early:
            warm_in = sbuf("warm_in", [P, 1], F32, early)
            nc.vector.memset(warm_in[:], 0.0)
            warm_out = sbuf("warm_out", [P, 1], F32, early)
            nc.scalar.activation(warm_out[:], warm_in[:], ACT.Sigmoid)

        late = ctx.enter_context(tc.tile_pool(name="late", bufs=1))
        wo_raw = sbuf("wo_raw", [P, PACK, R], F32, late)
        nc.sync.dma_start(wo_raw[:], wo.rearrange("(p t) r -> p t r", t=PACK))
        dy_raw = sbuf("dy_raw", [P, PACK, G], F32, late)
        nc.sync.dma_start(dy_raw[:], dy.rearrange("(p t) g -> p t g", t=PACK))
        x_view = xrows.rearrange("(p b) c -> p b c", b=PACK)
        x_raw = [sbuf("x_raw%d" % b, [P, T], F32, late) for b in range(PACK)]
        nc.sync.dma_start(x_raw[2][:], x_view[:, 2, :])
        js_cols = sbuf("js_cols", [P, PACK], F32, late)
        nc.gpsimd.dma_start(js_cols[:], js.rearrange("o (p t) -> (o p) t", t=PACK))
        for b in (0, 1, 3):
            nc.sync.dma_start(x_raw[b][:], x_view[:, b, :])
        old_sb = sbuf("old_sb", [P, PACK, R], F32, late)
        nc.sync.dma_start(old_sb[:], old.rearrange("(p b) r -> p b r", b=PACK))

        ident = sbuf("ident", [P, P], F32)
        make_identity(nc, ident[:])

        w1_grouped = sbuf("w1_grouped", [P, R, PACK], BF16)
        interleave(w1_grouped, w1_raw)
        wo_grouped = sbuf("wo_grouped", [P, R, PACK], BF16)
        interleave(wo_grouped, wo_raw)
        dy_grouped = sbuf("dy_grouped", [P, G, PACK], BF16)
        interleave(dy_grouped, dy_raw)

        HALF = J // 2
        a_ps = []
        for c in range(2):
            half_offsets = offsets[:, c * HALF // 16 : (c + 1) * HALF // 16]
            words_g = sbuf("words_g%d" % c, [P, HALF], U16)
            nc.vector.tensor_copy(words_g[:], words[:].indirect(half_offsets))
            plane_g = sbuf("plane_g%d" % c, [P, HALF], U8)
            nc.vector.tensor_copy(plane_g[:], plane[:].indirect(half_offsets))
            if c == 0:
                w1_q, w1_s = quantize("w1", w1_grouped[:].rearrange("p r t -> p (r t)"), R)
            bank = psum.tile([P, HALF], F32, name="a_ps%d" % c)
            nc.tensor.matmul_mx(
                out=bank[:], lhsT=w1_q, lhsT_scale=w1_s, rhs=words_g[:].bitcast(FP4X4), rhs_scale=plane_g[:],
                start=True, stop=True,
            )
            a_ps.append(bank)

        wo_q, wo_s = quantize("wo", wo_grouped[:].rearrange("p r t -> p (r t)"), R)
        dy_q, dy_s = quantize("dy", dy_grouped[:].rearrange("p g t -> p (g t)"), G)
        c0_ps = psum.tile([P, G], F32, name="c0_ps")
        nc.tensor.matmul_mx(out=c0_ps[:], lhsT=wo_q, lhsT_scale=wo_s, rhs=dy_q, rhs_scale=dy_s, start=True, stop=True)

        def gather_x(b, after):
            xg = sbuf("xg%d" % b, [P, J], BF16, tag=after)
            nc.vector.tensor_copy(xg[:], x_raw[b][:].indirect(offsets[:]))
            return xg

        def turn_x(b, xg, xt, bank_tag=None):
            pairs = xg[:].bitcast(F32)
            xt_ps = psum.tile([P, 2, P], F32, name="xt_ps%d" % b, tag=bank_tag or "xt_ps%d" % b)
            for u in range(2):
                nc.tensor.transpose(xt_ps[:, u, :], pairs[:, u : J // 2 : 2], ident[:])
            nc.scalar.copy(
                xt.bitcast(F32).rearrange("p (k u) -> p k u", u=2),
                xt_ps[:].rearrange("p u k -> p k u"),
            )

        def twice(ap):
            return ap.rearrange("r (g e) -> r g e", e=1).broadcast_to([P, G, 2])

        def over_places(t):
            return t[:].rearrange("r (t g) e -> r t (g e)", t=1).broadcast_to([P, PACK, P])

        neg_steep = sbuf("neg_steep", [P, 1], F32)
        nc.gpsimd.tensor_scalar(neg_steep[:], steep_col[:], -1.0, 0.0, ALU.mult, ALU.add)
        p_t = sbuf("p_t", [P, PACK, P], F32, late, "dy_raw")
        h_t = sbuf("h_t", [P, PACK, P], F32)
        ph_t = sbuf("ph_t", [P, PACK, P], F32)
        z = sbuf("z", [P, G], F32)
        s_ph = sbuf("s_ph", [P, G], F32)
        rz = sbuf("rz", [P, G], F32)
        for c in range(2):
            cols = slice(c * P // 2, (c + 1) * P // 2)
            groups = slice(c * G // 2, (c + 1) * G // 2)
            a_dealt = a_ps[c][:].rearrange("r (s t) -> r t s", t=PACK)
            nc.scalar.activation(p_t[:, :, cols], a_dealt, ACT.Sigmoid, scale=steep_col[:])
            nc.scalar.activation(h_t[:, :, cols], a_dealt, ACT.Tanh)
            nc.vector.tensor_reduce(
                z[:, groups], p_t[:, :, cols].rearrange("r t (g e) -> r g t e", e=2), AXIS.XY, ALU.add
            )
            nc.vector.scalar_tensor_tensor(
                ph_t[:, :, cols], p_t[:, :, cols], steep_col[:], h_t[:, :, cols], ALU.mult, ALU.mult
            )
            nc.vector.reciprocal(rz[:, groups], z[:, groups])
            nc.vector.tensor_reduce(
                s_ph[:, groups], ph_t[:, :, cols].rearrange("r t (g e) -> r g t e", e=2), AXIS.XY, ALU.add
            )
        hh_t = sbuf("hh_t", [P, PACK, P], F32)
        nc.scalar.activation(hh_t[:], h_t[:], ACT.Square)
        nsh_t = sbuf("nsh_t", [P, PACK, P], F32)
        nc.scalar.activation(nsh_t[:], h_t[:], ACT.Copy, scale=neg_steep[:])
        x2_bf16 = sbuf("x2_bf16", [P, T], BF16, tag="words_g1")
        nc.scalar.activation(x2_bf16[:], x_raw[2][:], ACT.Copy)

        ne1 = sbuf("ne1", [P, G, 2], F32)
        nc.vector.scalar_tensor_tensor(ne1[:], twice(c0_ps[:]), -1.0, twice(rz[:]), ALU.mult, ALU.mult)
        ms = sbuf("ms", [P, G, 2], F32)
        nc.vector.scalar_tensor_tensor(ms[:], twice(s_ph[:]), -1.0, twice(rz[:]), ALU.mult, ALU.mult)
        pe = sbuf("pe", [P, PACK, P], F32)
        nc.vector.tensor_tensor(pe[:], p_t[:], over_places(ne1), ALU.mult)
        term = sbuf("term", [P, PACK, P], F32)
        nc.vector.scalar_tensor_tensor(term[:], p_t[:], -1.0, over_places(ms), ALU.add, ALU.mult)

        xg0 = gather_x(0, "s_ph")
        pe_ps = psum.tile([P, PACK, R], F32, name="pe_ps", tag="a_ps0")
        for t in range(PACK):
            nc.tensor.transpose(pe_ps[:, t, :], pe[:, t, :], ident[:])
        y_ps = psum.tile([P, PACK, R], F32, name="y_ps", tag="a_ps1")
        addends = [hh_t, ph_t, nsh_t, term]
        for i, addend in enumerate(addends):
            for t in range(PACK):
                nc.tensor.matmul(
                    y_ps[:, t, :], addend[:, t, :], ident[:], is_transpose=True,
                    start=i == 0 and t == 0, stop=i == len(addends) - 1 and t == PACK - 1,
                )
        factor = sbuf("factor", [P, PACK, R], F32)
        for t in range(PACK):
            nc.scalar.activation(factor[:, t, :], pe_ps[:, t, :], ACT.Copy, scale=js_cols[:, t : t + 1])


        xg2 = sbuf("xg2", [P, J], BF16, tag="pe")
        nc.scalar.activation(xg2[:], x2_bf16[:].indirect(offsets[:]), ACT.Copy)

        xt01 = sbuf("xt01", [P, 2 * J], BF16)
        xt2 = sbuf("xt2", [P, J], BF16)
        xt3 = sbuf("xt3", [P, J], BF16)
        turn_x(0, xg0, xt01[:, 0:J])
        turn_x(1, gather_x(1, "ms"), xt01[:, J : 2 * J])
        turn_x(2, xg2, xt2[:], "a_ps0")
        gt = sbuf("gt", [P, R, PACK], BF16, late, "x_raw1")
        nc.vector.scalar_tensor_tensor(
            gt[:], y_ps[:].rearrange("p t r -> p r t"), -1.0, factor[:].rearrange("p t r -> p r t"), ALU.add, ALU.mult
        )
        turn_x(3, gather_x(3, "ne1"), xt3[:])
        gt_q, gt_s = quantize("gt", gt[:].rearrange("p r t -> p (r t)"), R, late, "x_raw3")
        x01_q, x01_s = quantize("x01", xt01[:], 2 * P, late, "x_raw1")
        x2_q, x2_s = quantize("x2", xt2[:], P, keep, "xt01")
        x3_q, x3_s = quantize("x3", xt3[:], P)

        out_view = out.rearrange("(p b) r -> p b r", b=PACK)
        gw_a = psum.tile([P, PACK - 1, R], F32, name="gw_a")
        for b, (x_q, x_s) in enumerate([(x01_q[:, 0:P], x01_s[:, 0:P]), (x01_q[:, P:], x01_s[:, P:]), (x2_q, x2_s)]):
            nc.tensor.matmul_mx(
                out=gw_a[:, b, :], lhsT=x_q, lhsT_scale=x_s, rhs=gt_q, rhs_scale=gt_s, start=True, stop=True
            )
        gw_b = psum.tile([P, R], F32, name="gw_b")
        nc.tensor.matmul_mx(out=gw_b[:], lhsT=x3_q, lhsT_scale=x3_s, rhs=gt_q, rhs_scale=gt_s, start=True, stop=True)
        res_a = sbuf("res_a", [P, PACK - 1, R], F32, tag="xt3")
        nc.vector.tensor_tensor(res_a[:], gw_a[:], old_sb[:, 0 : PACK - 1, :], ALU.add)
        nc.sync.dma_start(out_view[:, 0 : PACK - 1, :], res_a[:])
        res_b = sbuf("res_b", [P, R], F32)
        nc.vector.tensor_tensor(res_b[:], gw_b[:], old_sb[:, PACK - 1, :], ALU.add)
        nc.scalar.dma_start(out_view[:, PACK - 1, :], res_b[:])
